import numpy as np
import ml_dtypes


def mxq(x, axis, fmt="e4m3"):
    dtype, down = {"e4m3": (ml_dtypes.float8_e4m3fn, 7), "e5m2": (ml_dtypes.float8_e5m2, 14)}[fmt]
    v = np.moveaxis(np.asarray(x, np.float32).astype(ml_dtypes.bfloat16).astype(np.float64), axis, -1)
    blocks = v.reshape(v.shape[:-1] + (-1, 32))
    amax = np.abs(blocks).max(-1, keepdims=True)
    byte = np.maximum(np.where(amax > 0, np.frexp(amax)[1] - 1 + 127, 0) - down, 1)
    scale = np.exp2(byte - 127.0)
    codes = (blocks / scale).astype(np.float32).astype(dtype).astype(np.float64)
    return np.moveaxis((codes * scale).reshape(v.shape), -1, axis)


WIDE = False


def mx_kscale(k):
    if not WIDE:
        return np.ones(k)
    levels = np.array([10, -10, 5, -5, 0])
    if k % 512:
        return np.exp2(np.random.permutation(np.resize(levels, k // 32))).repeat(32)
    a = np.empty((k // 512, 16))
    for p in range(k // 512):
        a[p, :8] = np.random.permutation(np.resize(levels, 8))
        for g in range(8):
            far = levels[np.abs(levels - a[p, g]) >= 10]
            a[p, g + 8] = far[np.random.randint(len(far))]
    return np.exp2(a.ravel()).repeat(32)


def f64(x):
    return np.asarray(x).astype(np.float64)


def striped(idx):
    return np.tile(np.asarray(idx).reshape(-1, 16).T, (8, 1)).astype(np.uint16)


def unstriped(offs):
    return offs[:16].T.reshape(-1).astype(np.int64)


E2M1 = np.array([0.0, 0.5, 1.0, 1.5, 2.0, 3.0, 4.0, 6.0, -0.0, -0.5, -1.0, -1.5, -2.0, -3.0, -4.0, -6.0])


def pack_weight(w, fmt):
    k, n = w.shape
    w = f64(np.asarray(w, np.float32).astype(ml_dtypes.bfloat16)).reshape(k // 32, 32, n)
    amax = np.abs(w).max(1)
    if fmt == "e4m3":
        byte = np.frexp(amax)[1] - 1 + 127 - 7
    else:
        mant, ex = np.frexp(amax / 6.0)
        byte = np.where(mant > 0.5, ex, ex - 1) + 127
    byte = np.clip(np.where(amax > 0, byte, 1), 1, 254)
    scaled = (w * np.exp2(127.0 - byte)[:, None, :]).reshape(k, n).astype(np.float32)
    by_word = np.ascontiguousarray(scaled.reshape(k // 512, 128, 4, n).transpose(0, 1, 3, 2))
    if fmt == "e4m3":
        words = by_word.astype(ml_dtypes.float8_e4m3fn).view(np.uint8)
    else:
        c = by_word.astype(ml_dtypes.float4_e2m1fn).view(np.uint8) & 0xF
        words = (c[..., 0::2] | (c[..., 1::2] << 4)).reshape(k // 512, 128, 2 * n)
    return np.ascontiguousarray(words), np.ascontiguousarray(byte.astype(np.uint8).reshape(k // 512, 16, n))


def unpack_weight(words, scales, fmt):
    g, _, n = scales.shape
    words = np.ascontiguousarray(words).reshape(g, 128, n, -1)
    if fmt == "e4m3":
        vals = words.view(ml_dtypes.float8_e4m3fn).astype(np.float64)
    else:
        nib = np.empty((g, 128, n, 4), np.uint8)
        nib[..., 0::2] = words & 0xF
        nib[..., 1::2] = words >> 4
        vals = E2M1[nib]
    vals = vals * np.repeat(np.exp2(scales.astype(np.float64) - 127.0), 8, axis=1)[..., None]
    return vals.transpose(0, 1, 3, 2).reshape(g * 512, n)


D, T, I, J, U, E, M = 512, 2048, 512, 256, 1024, 512, 1024


def setup_inputs():
    n = np.random.standard_normal
    idx = np.random.permutation(T)[:I]
    idx2 = np.random.permutation(U)[:J]
    idx3 = np.random.permutation(U)[:J]
    idx4 = np.random.permutation(M)[:J]
    fd = mx_kscale(D)
    fi = mx_kscale(I)
    ti = np.ones(T)
    ti[idx] = fi
    keysp = pack_weight(n((D, T)) / fd[:, None], "e4m3")
    return {
        "keys_words": keysp[0],
        "keys_scales": keysp[1],
        "notes": (n((D, U)) * 1.0 / np.sqrt(D) * fd[:, None]).astype(np.float32),
        "rowf": (np.random.uniform(0.02, 0.08, (I, 1)) * fi[:, None]).astype(np.float32),
        "vals": (n((E, T)) / ti).astype(np.float32),
        "held": (n((E, M))).astype(np.float32),
        "hgain": np.tile(np.random.uniform(0.5, 2.0, M), (128, 1)).astype(np.float32),
        "offs": striped(idx),
        "offs2": striped(idx2),
        "offs3": striped(idx3),
        "offs4": striped(idx4),
    }


def reference(keys_words, keys_scales, notes, rowf, vals, held, hgain, offs, offs2, offs3, offs4):
    idx = unstriped(offs)
    idx2 = unstriped(offs2)
    idx3 = unstriped(offs3)
    idx4 = unstriped(offs4)
    keysu = unpack_weight(keys_words, keys_scales, "e4m3")
    keysidxg = keysu[:, idx]
    notesq = mxq(f64(notes), 0, "e4m3")
    g1 = keysidxg.T @ notesq
    g9 = g1[:, idx2] - g1[:, idx3]
    g0 = np.maximum(g9, 0.0)
    gr1 = g0 * f64(rowf)
    vt1 = f64(vals)[:, idx].T
    vt1q = mxq(vt1, 0, "e4m3")
    gr1q = mxq(gr1, 0, "e4m3")
    o = vt1q.T @ gr1q
    y = f64(held)[:, idx4] + o * f64(hgain)[:1][:, idx4]
    return y

@@ -1,0 +1,179 @@
+from contextlib import ExitStack
+
+import concourse.mybir as mybir
+from concourse.masks import make_identity
+
+D, T, I, J, U, E, M = 512, 2048, 512, 256, 1024, 512, 1024
+FLOPS = 2 * D * I * U + 2 * I * E * J
+BYTES = D * T + D * T // 32 + 4 * (D * U + I + E * T + E * M + M + E * J) + 2 * 128 * (I + 3 * J) // 16
+
+F32 = mybir.dt.float32
+BF16 = mybir.dt.bfloat16
+I32 = mybir.dt.int32
+U32 = mybir.dt.uint32
+U16 = mybir.dt.uint16
+U8 = mybir.dt.uint8
+FP8X4 = mybir.dt.float8_e4m3fn_x4
+ALU = mybir.AluOpType
+COPY = mybir.ActivationFunctionType.Copy
+
+P = 128
+PACK = 4
+BANK = 512
+CHUNK = 256
+CHUNKS = U // CHUNK
+BLOCKS = E // P
+GAINS = M // P
+
+
+def tile_attend_tab_looked_merge_kernel(tc, keys_words, keys_scales, notes, rowf, vals, held, hgain,
+                                         offs, offs2, offs3, offs4, out):
+    nc = tc.nc
+    with ExitStack() as ctx:
+        lists = ctx.enter_context(tc.tile_pool(name="lists", bufs=1))
+        sb = ctx.enter_context(tc.tile_pool(name="sb", bufs=1))
+        psum = ctx.enter_context(tc.psum_pool(name="psum", bufs=8))
+
+        idx = lists.tile([P, I // 16], U16, name="idx")
+        idx2 = lists.tile([P, J // 16], U16, name="idx2")
+        idx3 = lists.tile([P, J // 16], U16, name="idx3")
+        idx4 = lists.tile([P, J // 16], U16, name="idx4")
+
+        notes_by_word = notes.rearrange("(p t) u -> p t u", t=PACK)
+        notes_raw = [sb.tile([P, PACK, CHUNK], F32, name=f"notes_raw{c}") for c in range(CHUNKS)]
+
+        def load_notes(c):
+            nc.sync.dma_start(notes_raw[c][:], notes_by_word[:, :, c * CHUNK : (c + 1) * CHUNK])
+
+        gain_row = sb.tile([P, GAINS], F32, name="gain_row")
+        identity = sb.tile([P, P], F32, name="identity")
+        make_identity(nc, identity[:])
+
+        load_notes(0)
+        key_scale_rows = sb.tile([P, T // 4], I32, name="key_scale_rows")
+        for q in range(4):
+            nc.sync.dma_start(key_scale_rows[32 * q : 32 * q + 4, :], keys_scales[0, 4 * q : 4 * q + 4, :].bitcast(I32))
+        nc.sync.dma_start(idx[:], offs)
+        nc.sync.dma_start(gain_row[:], hgain[0].rearrange("(p c) -> p c", c=GAINS))
+        key_word_pool = sb.tile([P, T], I32, name="key_word_pool", align_bytes=64)
+        nc.sync.dma_start(key_word_pool[:], keys_words[0].rearrange("p n t -> p (n t)").bitcast(I32))
+        load_notes(1)
+        nc.sync.dma_start(idx4[:], offs4)
+        load_notes(2)
+        load_notes(3)
+        nc.sync.dma_start(idx3[:], offs3)
+        nc.sync.dma_start(idx2[:], offs2)
+        row_factor = sb.tile([P, PACK], F32, name="row_factor")
+        nc.sync.dma_start(row_factor[:], rowf.rearrange("(p r) o -> p (r o)", r=PACK))
+        val_pool = [sb.tile([P, T], F32, name=f"val_pool{b}") for b in range(BLOCKS)]
+        held_pool = [sb.tile([P, M], F32, name=f"held_pool{b}") for b in range(BLOCKS)]
+        for b in range(BLOCKS):
+            nc.sync.dma_start(val_pool[b][:], vals[b * P : (b + 1) * P, :])
+        for b in range(BLOCKS):
+            nc.sync.dma_start(held_pool[b][:], held[b * P : (b + 1) * P, :])
+
+        key_scale_pool = sb.tile([P, T], U8, name="key_scale_pool", align_bytes=64)
+        nc.vector.memset(key_scale_pool[:].bitcast(I32), 0)
+        for q in range(4):
+            nc.vector.tensor_copy(key_scale_pool[32 * q : 32 * q + 4, :].bitcast(I32), key_scale_rows[32 * q : 32 * q + 4, :])
+        key_scales = sb.tile([P, PACK, P], U8, name="key_scales", align_bytes=64)
+        key_words = sb.tile([P, PACK, P], U32, name="key_words", align_bytes=64)
+        nc.vector.tensor_copy(key_scales[:].rearrange("p r s -> p s r"), key_scale_pool[:].indirect(idx[:]))
+        nc.vector.tensor_copy(key_words[:].rearrange("p r s -> p s r"),
+                              key_word_pool[:].bitcast(U32).indirect(idx[:]))
+
+        note_words, note_scales = [], []
+        for c in range(CHUNKS):
+            grouped = sb.tile([P, CHUNK, PACK], BF16, name=f"notes_grouped{c}", align_bytes=64)
+            dst = grouped[:].rearrange("p (c i) t -> p c t i", i=4)
+            src = notes_raw[c][:].rearrange("p t (c i) -> p c t i", i=4)
+            if c < 2:
+                nc.scalar.copy(dst, src)
+            else:
+                nc.vector.tensor_copy(dst, src)
+            words = sb.tile([P, CHUNK], U32, name=f"note_words{c}", align_bytes=64)
+            scales = sb.tile([P, CHUNK], U8, name=f"note_scales{c}", align_bytes=64)
+            nc.vector.quantize_mx(out=words[:].bitcast(FP8X4), scales=scales[:],
+                                  in_=grouped[:].rearrange("p u t -> p (u t)"))
+            note_words.append(words)
+            note_scales.append(scales)
+
+        gain_pool = sb.tile([P, M], F32, name="gain_pool")
+        for half in range(2):
+            spread = psum.tile([P, PACK, P], F32, name="spread", tag="bank")
+            for k in range(PACK):
+                c = PACK * half + k
+                nc.tensor.transpose(spread[:, k, :], gain_row[:, c : c + 1].to_broadcast([P, P]), identity[:])
+            nc.scalar.copy(gain_pool[:].rearrange("x (n c) -> x n c", c=GAINS)[:, :, PACK * half : PACK * (half + 1)],
+                           spread[:].rearrange("x k n -> x n k"))
+        gain = sb.tile([P, J], F32, name="gain")
+        nc.vector.tensor_copy(gain[:], gain_pool[:].indirect(idx4[:]))
+
+        g1 = [sb.tile([P, U], F32, name=f"g1_{r}") for r in range(PACK)]
+        for c in range(CHUNKS):
+            for r in range(PACK):
+                acc = psum.tile([P, CHUNK], F32, name="g1_acc", tag="bank")
+                nc.tensor.matmul_mx(out=acc[:], lhsT=key_words[:, r, :].bitcast(FP8X4), lhsT_scale=key_scales[:, r, :],
+                                    rhs=note_words[c][:].bitcast(FP8X4), rhs_scale=note_scales[c][:],
+                                    start=True, stop=True)
+                dst = g1[r][:, c * CHUNK : (c + 1) * CHUNK]
+                if c >= 2 and r < 2:
+                    nc.vector.tensor_copy(dst, acc[:])
+                else:
+                    nc.scalar.copy(dst, acc[:])
+
+        g9 = sb.tile([P, PACK, J], F32, name="g9")
+        for r in range(PACK):
+            minus = sb.tile([P, J], F32, name=f"minus{r}", tag=f"picked{r}")
+            if r < 2:
+                nc.vector.tensor_copy(minus[:], g1[r][:].indirect(idx3[:]))
+            else:
+                nc.scalar.activation(minus[:], g1[r][:].indirect(idx3[:]), COPY)
+            nc.vector.tensor_tensor(g9[:, r, :], g1[r][:].indirect(idx2[:]), minus[:], ALU.subtract)
+        gr1 = sb.tile([P, J, PACK], BF16, name="gr1", align_bytes=64)
+        nc.vector.scalar_tensor_tensor(out=gr1[:], in0=g9[:].rearrange("p r j -> p j r"), scalar=0.0,
+                                       in1=row_factor[:].unsqueeze(1).to_broadcast([P, J, PACK]),
+                                       op0=ALU.max, op1=ALU.mult)
+        gr1_words = sb.tile([P, J], U32, name="gr1_words", align_bytes=64)
+        gr1_scales = sb.tile([P, J], U8, name="gr1_scales", align_bytes=64)
+        nc.vector.quantize_mx(out=gr1_words[:].bitcast(FP8X4), scales=gr1_scales[:],
+                              in_=gr1[:].rearrange("p j r -> p (j r)"))
+
+        gained = []
+        for group in ((0, 1), (2, 3)):
+            n = len(group)
+            turned = psum.tile([P, n, 2, P], F32, name="val_turned", tag="bank")
+            for k, b in enumerate(group):
+                picked = sb.tile([P, I], BF16, name=f"val_picked{b}", tag=f"picked{b}")
+                nc.scalar.activation(picked[:], val_pool[b][:].indirect(idx[:]), COPY)
+                twos = picked[:].bitcast(F32)
+                for h in range(2):
+                    nc.tensor.transpose(turned[:, k, h, :], twos[:, h : I // 2 : 2], identity[:])
+            vt1 = sb.tile([P, n * P, PACK], BF16, name=f"vt1_{group[0]}", align_bytes=64)
+            dst = vt1[:].bitcast(F32).rearrange("p (k e) h -> p k e h", k=n)
+            if group[0] == 0:
+                nc.vector.tensor_copy(dst, turned[:].rearrange("p k h e -> p k e h"))
+            else:
+                nc.scalar.copy(dst, turned[:].rearrange("p k h e -> p k e h"))
+            words = sb.tile([P, n * P], U32, name=f"val_words{group[0]}", align_bytes=64)
+            scales = sb.tile([P, n * P], U8, name=f"val_scales{group[0]}", align_bytes=64)
+            nc.vector.quantize_mx(out=words[:].bitcast(FP8X4), scales=scales[:],
+                                  in_=vt1[:].rearrange("p e t -> p (e t)"))
+            acc = psum.tile([P, n, J], F32, name="o_acc", tag="bank")
+            for k in range(n):
+                nc.tensor.matmul_mx(out=acc[:, k, :], lhsT=words[:, k * P : (k + 1) * P].bitcast(FP8X4),
+                                    lhsT_scale=scales[:, k * P : (k + 1) * P],
+                                    rhs=gr1_words[:].bitcast(FP8X4), rhs_scale=gr1_scales[:], start=True, stop=True)
+            product = sb.tile([P, n, J], F32, name=f"gained{group[0]}")
+            nc.vector.tensor_tensor(product[:], acc[:], gain[:].unsqueeze(1).to_broadcast([P, n, J]), ALU.mult)
+            gained += [product[:, k, :] for k in range(n)]
+
+        kept = sb.tile([P, BLOCKS - 1, J], F32, name="held_picked", tag=f"picked{BLOCKS - 1}")
+        for b in range(BLOCKS):
+            result = sb.tile([P, J], F32, name=f"result{b}")
+            if b < 3:
+                nc.scalar.activation(kept[:, b, :], held_pool[b][:].indirect(idx4[:]), COPY)
+                nc.vector.tensor_tensor(result[:], kept[:, b, :], gained[b], ALU.add)
+            else:
+                nc.vector.tensor_tensor(result[:], held_pool[b][:].indirect(idx4[:]), gained[b], ALU.add)
+            nc.sync.dma_start(out[b * P : (b + 1) * P, :], result[:])

@@ -40,7 +40,7 @@ def tile_attend_tab_looked_merge_kernel(tc, keys_words, keys_scales, notes, rowf
         idx4 = lists.tile([P, J // 16], U16, name="idx4")
 
         notes_by_word = notes.rearrange("(p t) u -> p t u", t=PACK)
-        notes_raw = [sb.tile([P, PACK, CHUNK], F32, name=f"notes_raw{c}") for c in range(CHUNKS)]
+        notes_raw = [sb.tile([P, PACK, CHUNK], F32, name=f"notes_raw{c}", tag=f"notes_raw{c}", align_bytes=64) for c in range(CHUNKS)]
 
         def load_notes(c):
             nc.sync.dma_start(notes_raw[c][:], notes_by_word[:, :, c * CHUNK : (c + 1) * CHUNK])
@@ -49,18 +49,16 @@ def tile_attend_tab_looked_merge_kernel(tc, keys_words, keys_scales, notes, rowf
         identity = sb.tile([P, P], F32, name="identity")
         make_identity(nc, identity[:])
 
-        load_notes(0)
         key_scale_rows = sb.tile([P, T // 4], I32, name="key_scale_rows")
+        nc.scalar.dma_start(gain_row[:], hgain[0].rearrange("(p c) -> p c", c=GAINS))
         for q in range(4):
             nc.sync.dma_start(key_scale_rows[32 * q : 32 * q + 4, :], keys_scales[0, 4 * q : 4 * q + 4, :].bitcast(I32))
         nc.sync.dma_start(idx[:], offs)
-        nc.sync.dma_start(gain_row[:], hgain[0].rearrange("(p c) -> p c", c=GAINS))
-        key_word_pool = sb.tile([P, T], I32, name="key_word_pool", align_bytes=64)
-        nc.sync.dma_start(key_word_pool[:], keys_words[0].rearrange("p n t -> p (n t)").bitcast(I32))
-        load_notes(1)
         nc.sync.dma_start(idx4[:], offs4)
-        load_notes(2)
-        load_notes(3)
+        key_word_pool = sb.tile([P, T], I32, name="key_word_pool", tag="key_word_pool", align_bytes=64)
+        nc.sync.dma_start(key_word_pool[:], keys_words[0].rearrange("p n t -> p (n t)").bitcast(I32))
+        for c in range(CHUNKS):
+            load_notes(c)
         nc.sync.dma_start(idx3[:], offs3)
         nc.sync.dma_start(idx2[:], offs2)
         row_factor = sb.tile([P, PACK], F32, name="row_factor")
@@ -82,12 +80,24 @@ def tile_attend_tab_looked_merge_kernel(tc, keys_words, keys_scales, notes, rowf
         nc.vector.tensor_copy(key_words[:].rearrange("p r s -> p s r"),
                               key_word_pool[:].bitcast(U32).indirect(idx[:]))
 
+        gain_pool = sb.tile([P, M], F32, name="gain_pool", tag="gain_pool", align_bytes=64)
+        for half in range(2):
+            spread = psum.tile([P, PACK, P], F32, name="spread", tag="bank")
+            for k in range(PACK):
+                c = PACK * half + k
+                nc.tensor.transpose(spread[:, k, :], gain_row[:, c : c + 1].to_broadcast([P, P]), identity[:])
+            nc.scalar.copy(gain_pool[:].rearrange("x (n c) -> x n c", c=GAINS)[:, :, PACK * half : PACK * (half + 1)],
+                           spread[:].rearrange("x k n -> x n k"))
+        gain = sb.tile([P, J], F32, name="gain")
+        nc.scalar.activation(gain[:], gain_pool[:].indirect(idx4[:]), COPY)
+
+        grouped_tags = ("key_word_pool", "gain_pool", "notes_raw1", "gain_pool")
         note_words, note_scales = [], []
         for c in range(CHUNKS):
-            grouped = sb.tile([P, CHUNK, PACK], BF16, name=f"notes_grouped{c}", align_bytes=64)
+            grouped = sb.tile([P, CHUNK, PACK], BF16, name=f"notes_grouped{c}", tag=grouped_tags[c], align_bytes=64)
             dst = grouped[:].rearrange("p (c i) t -> p c t i", i=4)
             src = notes_raw[c][:].rearrange("p t (c i) -> p c t i", i=4)
-            if c < 2:
+            if c == 1:
                 nc.scalar.copy(dst, src)
             else:
                 nc.vector.tensor_copy(dst, src)
@@ -98,80 +108,74 @@ def tile_attend_tab_looked_merge_kernel(tc, keys_words, keys_scales, notes, rowf
             note_words.append(words)
             note_scales.append(scales)
 
-        gain_pool = sb.tile([P, M], F32, name="gain_pool")
-        for half in range(2):
-            spread = psum.tile([P, PACK, P], F32, name="spread", tag="bank")
-            for k in range(PACK):
-                c = PACK * half + k
-                nc.tensor.transpose(spread[:, k, :], gain_row[:, c : c + 1].to_broadcast([P, P]), identity[:])
-            nc.scalar.copy(gain_pool[:].rearrange("x (n c) -> x n c", c=GAINS)[:, :, PACK * half : PACK * (half + 1)],
-                           spread[:].rearrange("x k n -> x n k"))
-        gain = sb.tile([P, J], F32, name="gain")
-        nc.vector.tensor_copy(gain[:], gain_pool[:].indirect(idx4[:]))
-
         g1 = [sb.tile([P, U], F32, name=f"g1_{r}") for r in range(PACK)]
-        for c in range(CHUNKS):
+        for half in range(U // BANK):
+            accs = [psum.tile([P, BANK], F32, name="g1_acc", tag="bank") for r in range(PACK)]
+            for k in range(BANK // CHUNK):
+                c = half * (BANK // CHUNK) + k
+                for r in range(PACK):
+                    nc.tensor.matmul_mx(out=accs[r][:, k * CHUNK : (k + 1) * CHUNK],
+                                        lhsT=key_words[:, r, :].bitcast(FP8X4), lhsT_scale=key_scales[:, r, :],
+                                        rhs=note_words[c][:].bitcast(FP8X4), rhs_scale=note_scales[c][:],
+                                        start=True, stop=True)
             for r in range(PACK):
-                acc = psum.tile([P, CHUNK], F32, name="g1_acc", tag="bank")
-                nc.tensor.matmul_mx(out=acc[:], lhsT=key_words[:, r, :].bitcast(FP8X4), lhsT_scale=key_scales[:, r, :],
-                                    rhs=note_words[c][:].bitcast(FP8X4), rhs_scale=note_scales[c][:],
-                                    start=True, stop=True)
-                dst = g1[r][:, c * CHUNK : (c + 1) * CHUNK]
-                if c >= 2 and r < 2:
-                    nc.vector.tensor_copy(dst, acc[:])
+                dst = g1[r][:, half * BANK : (half + 1) * BANK]
+                if half == 1 and r < 2:
+                    nc.vector.tensor_copy(dst, accs[r][:])
                 else:
-                    nc.scalar.copy(dst, acc[:])
+                    nc.scalar.copy(dst, accs[r][:])
 
-        g9 = sb.tile([P, PACK, J], F32, name="g9")
+        gr1 = sb.tile([P, J, PACK], BF16, name="gr1", align_bytes=64)
         for r in range(PACK):
-            minus = sb.tile([P, J], F32, name=f"minus{r}", tag=f"picked{r}")
+            minus = sb.tile([P, J], F32, name=f"minus{r}", tag=f"minus{r}", align_bytes=64)
             if r < 2:
                 nc.vector.tensor_copy(minus[:], g1[r][:].indirect(idx3[:]))
             else:
                 nc.scalar.activation(minus[:], g1[r][:].indirect(idx3[:]), COPY)
-            nc.vector.tensor_tensor(g9[:, r, :], g1[r][:].indirect(idx2[:]), minus[:], ALU.subtract)
-        gr1 = sb.tile([P, J, PACK], BF16, name="gr1", align_bytes=64)
-        nc.vector.scalar_tensor_tensor(out=gr1[:], in0=g9[:].rearrange("p r j -> p j r"), scalar=0.0,
-                                       in1=row_factor[:].unsqueeze(1).to_broadcast([P, J, PACK]),
-                                       op0=ALU.max, op1=ALU.mult)
+            g9 = sb.tile([P, J], F32, name=f"g9_{r}", tag=f"g9_{r}", align_bytes=64)
+            nc.vector.tensor_tensor(g9[:], g1[r][:].indirect(idx2[:]), minus[:], ALU.subtract)
+            nc.vector.tensor_scalar(gr1[:, :, r], g9[:], 0.0, row_factor[:, r : r + 1], ALU.max, ALU.mult)
         gr1_words = sb.tile([P, J], U32, name="gr1_words", align_bytes=64)
         gr1_scales = sb.tile([P, J], U8, name="gr1_scales", align_bytes=64)
         nc.vector.quantize_mx(out=gr1_words[:].bitcast(FP8X4), scales=gr1_scales[:],
                               in_=gr1[:].rearrange("p j r -> p (j r)"))
 
-        gained = []
-        for group in ((0, 1), (2, 3)):
-            n = len(group)
+        def quantised_values(blocks, picked_tags, vt1_tag, copy):
+            n = len(blocks)
             turned = psum.tile([P, n, 2, P], F32, name="val_turned", tag="bank")
-            for k, b in enumerate(group):
-                picked = sb.tile([P, I], BF16, name=f"val_picked{b}", tag=f"picked{b}")
+            for k, b in enumerate(blocks):
+                picked = sb.tile([P, I], BF16, name=f"val_picked{b}", tag=picked_tags[k], align_bytes=64)
                 nc.scalar.activation(picked[:], val_pool[b][:].indirect(idx[:]), COPY)
                 twos = picked[:].bitcast(F32)
                 for h in range(2):
                     nc.tensor.transpose(turned[:, k, h, :], twos[:, h : I // 2 : 2], identity[:])
-            vt1 = sb.tile([P, n * P, PACK], BF16, name=f"vt1_{group[0]}", align_bytes=64)
-            dst = vt1[:].bitcast(F32).rearrange("p (k e) h -> p k e h", k=n)
-            if group[0] == 0:
-                nc.vector.tensor_copy(dst, turned[:].rearrange("p k h e -> p k e h"))
-            else:
-                nc.scalar.copy(dst, turned[:].rearrange("p k h e -> p k e h"))
-            words = sb.tile([P, n * P], U32, name=f"val_words{group[0]}", align_bytes=64)
-            scales = sb.tile([P, n * P], U8, name=f"val_scales{group[0]}", align_bytes=64)
+            vt1 = sb.tile([P, n * P, PACK], BF16, name=f"vt1_{blocks[0]}", tag=vt1_tag, align_bytes=64)
+            copy(vt1[:].bitcast(F32).rearrange("p (k e) h -> p k e h", k=n), turned[:].rearrange("p k h e -> p k e h"))
+            words = sb.tile([P, n * P], U32, name=f"val_words{blocks[0]}", align_bytes=64)
+            scales = sb.tile([P, n * P], U8, name=f"val_scales{blocks[0]}", align_bytes=64)
             nc.vector.quantize_mx(out=words[:].bitcast(FP8X4), scales=scales[:],
                                   in_=vt1[:].rearrange("p e t -> p (e t)"))
-            acc = psum.tile([P, n, J], F32, name="o_acc", tag="bank")
-            for k in range(n):
-                nc.tensor.matmul_mx(out=acc[:, k, :], lhsT=words[:, k * P : (k + 1) * P].bitcast(FP8X4),
-                                    lhsT_scale=scales[:, k * P : (k + 1) * P],
-                                    rhs=gr1_words[:].bitcast(FP8X4), rhs_scale=gr1_scales[:], start=True, stop=True)
-            product = sb.tile([P, n, J], F32, name=f"gained{group[0]}")
-            nc.vector.tensor_tensor(product[:], acc[:], gain[:].unsqueeze(1).to_broadcast([P, n, J]), ALU.mult)
-            gained += [product[:, k, :] for k in range(n)]
+            return [(words[:, k * P : (k + 1) * P], scales[:, k * P : (k + 1) * P]) for k in range(n)]
 
-        kept = sb.tile([P, BLOCKS - 1, J], F32, name="held_picked", tag=f"picked{BLOCKS - 1}")
+        vt1q = quantised_values((0, 1), ("gain_pool", "minus0"), "g9_2", nc.vector.tensor_copy)
+        vt1q += quantised_values((2,), ("minus1",), "g9_3", nc.vector.tensor_copy)
+        vt1q += quantised_values((3,), ("minus2",), "vt1_3", nc.scalar.copy)
+
+        gained = []
+        for pair in range(BLOCKS // 2):
+            acc = psum.tile([P, 2, J], F32, name="o_acc", tag="bank")
+            for k in range(2):
+                words, scales = vt1q[2 * pair + k]
+                nc.tensor.matmul_mx(out=acc[:, k, :], lhsT=words.bitcast(FP8X4), lhsT_scale=scales,
+                                    rhs=gr1_words[:].bitcast(FP8X4), rhs_scale=gr1_scales[:], start=True, stop=True)
+            product = sb.tile([P, 2, J], F32, name=f"gained{pair}")
+            nc.vector.tensor_tensor(product[:], acc[:], gain[:].unsqueeze(1).to_broadcast([P, 2, J]), ALU.mult)
+            gained += [product[:, 0, :], product[:, 1, :]]
+
+        kept = sb.tile([P, BLOCKS - 1, J], F32, name="held_picked", tag="minus2", align_bytes=64)
         for b in range(BLOCKS):
             result = sb.tile([P, J], F32, name=f"result{b}")
-            if b < 3:
+            if b < BLOCKS - 1:
                 nc.scalar.activation(kept[:, b, :], held_pool[b][:].indirect(idx4[:]), COPY)
                 nc.vector.tensor_tensor(result[:], kept[:, b, :], gained[b], ALU.add)
             else:

@@ -50,13 +50,14 @@ def tile_attend_tab_looked_merge_kernel(tc, keys_words, keys_scales, notes, rowf
         make_identity(nc, identity[:])
 
         key_scale_rows = sb.tile([P, T // 4], I32, name="key_scale_rows")
+        for f in range(4):
+            queue = nc.sync if f < 2 else nc.scalar
+            queue.dma_start(key_scale_rows[f:P:32, :], keys_scales[0, f:16:4, :].bitcast(I32))
         nc.scalar.dma_start(gain_row[:], hgain[0].rearrange("(p c) -> p c", c=GAINS))
-        for q in range(4):
-            nc.sync.dma_start(key_scale_rows[32 * q : 32 * q + 4, :], keys_scales[0, 4 * q : 4 * q + 4, :].bitcast(I32))
         nc.sync.dma_start(idx[:], offs)
-        nc.sync.dma_start(idx4[:], offs4)
         key_word_pool = sb.tile([P, T], I32, name="key_word_pool", tag="key_word_pool", align_bytes=64)
         nc.sync.dma_start(key_word_pool[:], keys_words[0].rearrange("p n t -> p (n t)").bitcast(I32))
+        nc.sync.dma_start(idx4[:], offs4)
         for c in range(CHUNKS):
             load_notes(c)
         nc.sync.dma_start(idx3[:], offs3)
@@ -172,12 +173,9 @@ def tile_attend_tab_looked_merge_kernel(tc, keys_words, keys_scales, notes, rowf
             nc.vector.tensor_tensor(product[:], acc[:], gain[:].unsqueeze(1).to_broadcast([P, 2, J]), ALU.mult)
             gained += [product[:, 0, :], product[:, 1, :]]
 
-        kept = sb.tile([P, BLOCKS - 1, J], F32, name="held_picked", tag="minus2", align_bytes=64)
+        kept = sb.tile([P, BLOCKS, J], F32, name="held_picked", tag="minus2", align_bytes=64)
         for b in range(BLOCKS):
             result = sb.tile([P, J], F32, name=f"result{b}")
-            if b < BLOCKS - 1:
-                nc.scalar.activation(kept[:, b, :], held_pool[b][:].indirect(idx4[:]), COPY)
-                nc.vector.tensor_tensor(result[:], kept[:, b, :], gained[b], ALU.add)
-            else:
-                nc.vector.tensor_tensor(result[:], held_pool[b][:].indirect(idx4[:]), gained[b], ALU.add)
+            nc.scalar.activation(kept[:, b, :], held_pool[b][:].indirect(idx4[:]), COPY)
+            nc.vector.tensor_tensor(result[:], kept[:, b, :], gained[b], ALU.add)
             nc.sync.dma_start(out[b * P : (b + 1) * P, :], result[:])

@@ -129,7 +129,7 @@ def tile_attend_tab_looked_merge_kernel(tc, keys_words, keys_scales, notes, rowf
         gr1 = sb.tile([P, J, PACK], BF16, name="gr1", align_bytes=64)
         for r in range(PACK):
             minus = sb.tile([P, J], F32, name=f"minus{r}", tag=f"minus{r}", align_bytes=64)
-            if r < 2:
+            if r < 3:
                 nc.vector.tensor_copy(minus[:], g1[r][:].indirect(idx3[:]))
             else:
                 nc.scalar.activation(minus[:], g1[r][:].indirect(idx3[:]), COPY)
@@ -141,7 +141,7 @@ def tile_attend_tab_looked_merge_kernel(tc, keys_words, keys_scales, notes, rowf
         nc.vector.quantize_mx(out=gr1_words[:].bitcast(FP8X4), scales=gr1_scales[:],
                               in_=gr1[:].rearrange("p j r -> p (j r)"))
 
-        def quantised_values(blocks, picked_tags, vt1_tag, copy):
+        def quantised_values(blocks, picked_tags, vt1_tag, words_tag, copy):
             n = len(blocks)
             turned = psum.tile([P, n, 2, P], F32, name="val_turned", tag="bank")
             for k, b in enumerate(blocks):
@@ -152,15 +152,15 @@ def tile_attend_tab_looked_merge_kernel(tc, keys_words, keys_scales, notes, rowf
                     nc.tensor.transpose(turned[:, k, h, :], twos[:, h : I // 2 : 2], identity[:])
             vt1 = sb.tile([P, n * P, PACK], BF16, name=f"vt1_{blocks[0]}", tag=vt1_tag, align_bytes=64)
             copy(vt1[:].bitcast(F32).rearrange("p (k e) h -> p k e h", k=n), turned[:].rearrange("p k h e -> p k e h"))
-            words = sb.tile([P, n * P], U32, name=f"val_words{blocks[0]}", align_bytes=64)
+            words = sb.tile([P, n * P], U32, name=f"val_words{blocks[0]}", tag=words_tag, align_bytes=64)
             scales = sb.tile([P, n * P], U8, name=f"val_scales{blocks[0]}", align_bytes=64)
             nc.vector.quantize_mx(out=words[:].bitcast(FP8X4), scales=scales[:],
                                   in_=vt1[:].rearrange("p e t -> p (e t)"))
             return [(words[:, k * P : (k + 1) * P], scales[:, k * P : (k + 1) * P]) for k in range(n)]
 
-        vt1q = quantised_values((0, 1), ("gain_pool", "minus0"), "g9_2", nc.vector.tensor_copy)
-        vt1q += quantised_values((2,), ("minus1",), "g9_3", nc.vector.tensor_copy)
-        vt1q += quantised_values((3,), ("minus2",), "vt1_3", nc.scalar.copy)
+        vt1q = quantised_values((0, 1), ("gain_pool", "minus0"), "g9_2", "val_words0", nc.vector.tensor_copy)
+        vt1q += quantised_values((2,), ("g9_0",), "g9_3", "val_words2", nc.vector.tensor_copy)
+        vt1q += quantised_values((3,), ("minus1",), "vt1_3", "g9_2", nc.scalar.copy)
 
         gained = []
         for pair in range(BLOCKS // 2):
@@ -173,7 +173,7 @@ def tile_attend_tab_looked_merge_kernel(tc, keys_words, keys_scales, notes, rowf
             nc.vector.tensor_tensor(product[:], acc[:], gain[:].unsqueeze(1).to_broadcast([P, 2, J]), ALU.mult)
             gained += [product[:, 0, :], product[:, 1, :]]
 
-        kept = sb.tile([P, BLOCKS, J], F32, name="held_picked", tag="minus2", align_bytes=64)
+        kept = sb.tile([P, BLOCKS, J], F32, name="held_picked", tag="minus1", align_bytes=64)
         for b in range(BLOCKS):
             result = sb.tile([P, J], F32, name=f"result{b}")
             nc.scalar.activation(kept[:, b, :], held_pool[b][:].indirect(idx4[:]), COPY)

from contextlib import ExitStack

import concourse.mybir as mybir
from concourse.masks import make_identity

D, T, I, J, U, E, M = 512, 2048, 512, 256, 1024, 512, 1024
FLOPS = 2 * D * I * U + 2 * I * E * J
BYTES = D * T + D * T // 32 + 4 * (D * U + I + E * T + E * M + M + E * J) + 2 * 128 * (I + 3 * J) // 16

F32 = mybir.dt.float32
BF16 = mybir.dt.bfloat16
I32 = mybir.dt.int32
U32 = mybir.dt.uint32
U16 = mybir.dt.uint16
U8 = mybir.dt.uint8
FP8X4 = mybir.dt.float8_e4m3fn_x4
ALU = mybir.AluOpType
COPY = mybir.ActivationFunctionType.Copy

P = 128
PACK = 4
BANK = 512
CHUNK = 256
CHUNKS = U // CHUNK
BLOCKS = E // P
GAINS = M // P


def tile_attend_tab_looked_merge_kernel(tc, keys_words, keys_scales, notes, rowf, vals, held, hgain,
                                         offs, offs2, offs3, offs4, out):
    nc = tc.nc
    with ExitStack() as ctx:
        lists = ctx.enter_context(tc.tile_pool(name="lists", bufs=1))
        sb = ctx.enter_context(tc.tile_pool(name="sb", bufs=1))
        psum = ctx.enter_context(tc.psum_pool(name="psum", bufs=8))

        idx = lists.tile([P, I // 16], U16, name="idx")
        idx2 = lists.tile([P, J // 16], U16, name="idx2")
        idx3 = lists.tile([P, J // 16], U16, name="idx3")
        idx4 = lists.tile([P, J // 16], U16, name="idx4")

        notes_by_word = notes.rearrange("(p t) u -> p t u", t=PACK)
        notes_raw = [sb.tile([P, PACK, CHUNK], F32, name=f"notes_raw{c}", tag=f"notes_raw{c}", align_bytes=64) for c in range(CHUNKS)]

        def load_notes(c):
            nc.sync.dma_start(notes_raw[c][:], notes_by_word[:, :, c * CHUNK : (c + 1) * CHUNK])

        gain_row = sb.tile([P, GAINS], F32, name="gain_row")
        identity = sb.tile([P, P], F32, name="identity")
        make_identity(nc, identity[:])

        key_scale_rows = sb.tile([P, T // 4], I32, name="key_scale_rows")
        for f in range(4):
            queue = nc.sync if f < 2 else nc.scalar
            queue.dma_start(key_scale_rows[f:P:32, :], keys_scales[0, f:16:4, :].bitcast(I32))
        nc.scalar.dma_start(gain_row[:], hgain[0].rearrange("(p c) -> p c", c=GAINS))
        nc.sync.dma_start(idx[:], offs)
        key_word_pool = sb.tile([P, T], I32, name="key_word_pool", tag="key_word_pool", align_bytes=64)
        nc.sync.dma_start(key_word_pool[:], keys_words[0].rearrange("p n t -> p (n t)").bitcast(I32))
        nc.sync.dma_start(idx4[:], offs4)
        for c in range(CHUNKS):
            load_notes(c)
        nc.sync.dma_start(idx3[:], offs3)
        nc.sync.dma_start(idx2[:], offs2)
        row_factor = sb.tile([P, PACK], F32, name="row_factor")
        nc.sync.dma_start(row_factor[:], rowf.rearrange("(p r) o -> p (r o)", r=PACK))
        val_pool = [sb.tile([P, T], F32, name=f"val_pool{b}") for b in range(BLOCKS)]
        held_pool = [sb.tile([P, M], F32, name=f"held_pool{b}") for b in range(BLOCKS)]
        for b in range(BLOCKS):
            nc.sync.dma_start(val_pool[b][:], vals[b * P : (b + 1) * P, :])
        for b in range(BLOCKS):
            nc.sync.dma_start(held_pool[b][:], held[b * P : (b + 1) * P, :])

        key_scale_pool = sb.tile([P, T], U8, name="key_scale_pool", align_bytes=64)
        nc.vector.memset(key_scale_pool[:].bitcast(I32), 0)
        for q in range(4):
            nc.vector.tensor_copy(key_scale_pool[32 * q : 32 * q + 4, :].bitcast(I32), key_scale_rows[32 * q : 32 * q + 4, :])
        key_scales = sb.tile([P, PACK, P], U8, name="key_scales", align_bytes=64)
        key_words = sb.tile([P, PACK, P], U32, name="key_words", align_bytes=64)
        nc.vector.tensor_copy(key_scales[:].rearrange("p r s -> p s r"), key_scale_pool[:].indirect(idx[:]))
        nc.vector.tensor_copy(key_words[:].rearrange("p r s -> p s r"),
                              key_word_pool[:].bitcast(U32).indirect(idx[:]))

        gain_pool = sb.tile([P, M], F32, name="gain_pool", tag="gain_pool", align_bytes=64)
        for half in range(2):
            spread = psum.tile([P, PACK, P], F32, name="spread", tag="bank")
            for k in range(PACK):
                c = PACK * half + k
                nc.tensor.transpose(spread[:, k, :], gain_row[:, c : c + 1].to_broadcast([P, P]), identity[:])
            nc.scalar.copy(gain_pool[:].rearrange("x (n c) -> x n c", c=GAINS)[:, :, PACK * half : PACK * (half + 1)],
                           spread[:].rearrange("x k n -> x n k"))
        gain = sb.tile([P, J], F32, name="gain")
        nc.scalar.activation(gain[:], gain_pool[:].indirect(idx4[:]), COPY)

        grouped_tags = ("key_word_pool", "gain_pool", "notes_raw1", "gain_pool")
        note_words, note_scales = [], []
        for c in range(CHUNKS):
            grouped = sb.tile([P, CHUNK, PACK], BF16, name=f"notes_grouped{c}", tag=grouped_tags[c], align_bytes=64)
            dst = grouped[:].rearrange("p (c i) t -> p c t i", i=4)
            src = notes_raw[c][:].rearrange("p t (c i) -> p c t i", i=4)
            if c == 1:
                nc.scalar.copy(dst, src)
            else:
                nc.vector.tensor_copy(dst, src)
            words = sb.tile([P, CHUNK], U32, name=f"note_words{c}", align_bytes=64)
            scales = sb.tile([P, CHUNK], U8, name=f"note_scales{c}", align_bytes=64)
            nc.vector.quantize_mx(out=words[:].bitcast(FP8X4), scales=scales[:],
                                  in_=grouped[:].rearrange("p u t -> p (u t)"))
            note_words.append(words)
            note_scales.append(scales)

        g1 = [sb.tile([P, U], F32, name=f"g1_{r}") for r in range(PACK)]
        for half in range(U // BANK):
            accs = [psum.tile([P, BANK], F32, name="g1_acc", tag="bank") for r in range(PACK)]
            for k in range(BANK // CHUNK):
                c = half * (BANK // CHUNK) + k
                for r in range(PACK):
                    nc.tensor.matmul_mx(out=accs[r][:, k * CHUNK : (k + 1) * CHUNK],
                                        lhsT=key_words[:, r, :].bitcast(FP8X4), lhsT_scale=key_scales[:, r, :],
                                        rhs=note_words[c][:].bitcast(FP8X4), rhs_scale=note_scales[c][:],
                                        start=True, stop=True)
            for r in range(PACK):
                dst = g1[r][:, half * BANK : (half + 1) * BANK]
                if half == 1 and r < 2:
                    nc.vector.tensor_copy(dst, accs[r][:])
                else:
                    nc.scalar.copy(dst, accs[r][:])

        gr1 = sb.tile([P, J, PACK], BF16, name="gr1", align_bytes=64)
        for r in range(PACK):
            minus = sb.tile([P, J], F32, name=f"minus{r}", tag=f"minus{r}", align_bytes=64)
            if r < 3:
                nc.vector.tensor_copy(minus[:], g1[r][:].indirect(idx3[:]))
            else:
                nc.scalar.activation(minus[:], g1[r][:].indirect(idx3[:]), COPY)
            g9 = sb.tile([P, J], F32, name=f"g9_{r}", tag=f"g9_{r}", align_bytes=64)
            nc.vector.tensor_tensor(g9[:], g1[r][:].indirect(idx2[:]), minus[:], ALU.subtract)
            nc.vector.tensor_scalar(gr1[:, :, r], g9[:], 0.0, row_factor[:, r : r + 1], ALU.max, ALU.mult)
        gr1_words = sb.tile([P, J], U32, name="gr1_words", align_bytes=64)
        gr1_scales = sb.tile([P, J], U8, name="gr1_scales", align_bytes=64)
        nc.vector.quantize_mx(out=gr1_words[:].bitcast(FP8X4), scales=gr1_scales[:],
                              in_=gr1[:].rearrange("p j r -> p (j r)"))

        def quantised_values(blocks, picked_tags, vt1_tag, words_tag, copy):
            n = len(blocks)
            turned = psum.tile([P, n, 2, P], F32, name="val_turned", tag="bank")
            for k, b in enumerate(blocks):
                picked = sb.tile([P, I], BF16, name=f"val_picked{b}", tag=picked_tags[k], align_bytes=64)
                nc.scalar.activation(picked[:], val_pool[b][:].indirect(idx[:]), COPY)
                twos = picked[:].bitcast(F32)
                for h in range(2):
                    nc.tensor.transpose(turned[:, k, h, :], twos[:, h : I // 2 : 2], identity[:])
            vt1 = sb.tile([P, n * P, PACK], BF16, name=f"vt1_{blocks[0]}", tag=vt1_tag, align_bytes=64)
            copy(vt1[:].bitcast(F32).rearrange("p (k e) h -> p k e h", k=n), turned[:].rearrange("p k h e -> p k e h"))
            words = sb.tile([P, n * P], U32, name=f"val_words{blocks[0]}", tag=words_tag, align_bytes=64)
            scales = sb.tile([P, n * P], U8, name=f"val_scales{blocks[0]}", align_bytes=64)
            nc.vector.quantize_mx(out=words[:].bitcast(FP8X4), scales=scales[:],
                                  in_=vt1[:].rearrange("p e t -> p (e t)"))
            return [(words[:, k * P : (k + 1) * P], scales[:, k * P : (k + 1) * P]) for k in range(n)]

        vt1q = quantised_values((0, 1), ("gain_pool", "minus0"), "g9_2", "val_words0", nc.vector.tensor_copy)
        vt1q += quantised_values((2,), ("g9_0",), "g9_3", "val_words2", nc.vector.tensor_copy)
        vt1q += quantised_values((3,), ("minus1",), "vt1_3", "g9_2", nc.scalar.copy)

        gained = []
        for pair in range(BLOCKS // 2):
            acc = psum.tile([P, 2, J], F32, name="o_acc", tag="bank")
            for k in range(2):
                words, scales = vt1q[2 * pair + k]
                nc.tensor.matmul_mx(out=acc[:, k, :], lhsT=words.bitcast(FP8X4), lhsT_scale=scales,
                                    rhs=gr1_words[:].bitcast(FP8X4), rhs_scale=gr1_scales[:], start=True, stop=True)
            product = sb.tile([P, 2, J], F32, name=f"gained{pair}")
            nc.vector.tensor_tensor(product[:], acc[:], gain[:].unsqueeze(1).to_broadcast([P, 2, J]), ALU.mult)
            gained += [product[:, 0, :], product[:, 1, :]]

        kept = sb.tile([P, BLOCKS, J], F32, name="held_picked", tag="minus1", align_bytes=64)
        for b in range(BLOCKS):
            result = sb.tile([P, J], F32, name=f"result{b}")
            nc.scalar.activation(kept[:, b, :], held_pool[b][:].indirect(idx4[:]), COPY)
            nc.vector.tensor_tensor(result[:], kept[:, b, :], gained[b], ALU.add)
            nc.sync.dma_start(out[b * P : (b + 1) * P, :], result[:])
